import numpy as np
import ml_dtypes


def mxq(x, axis, fmt="e4m3"):
    dtype, down = {"e4m3": (ml_dtypes.float8_e4m3fn, 7), "e5m2": (ml_dtypes.float8_e5m2, 14)}[fmt]
    v = np.moveaxis(np.asarray(x, np.float32).astype(ml_dtypes.bfloat16).astype(np.float64), axis, -1)
    blocks = v.reshape(v.shape[:-1] + (-1, 32))
    amax = np.abs(blocks).max(-1, keepdims=True)
    byte = np.maximum(np.where(amax > 0, np.frexp(amax)[1] - 1 + 127, 0) - down, 1)
    scale = np.exp2(byte - 127.0)
    codes = (blocks / scale).astype(np.float32).astype(dtype).astype(np.float64)
    return np.moveaxis((codes * scale).reshape(v.shape), -1, axis)


WIDE = False


def mx_kscale(k):
    if not WIDE:
        return np.ones(k)
    levels = np.array([10, -10, 5, -5, 0])
    if k % 512:
        return np.exp2(np.random.permutation(np.resize(levels, k // 32))).repeat(32)
    a = np.empty((k // 512, 16))
    for p in range(k // 512):
        a[p, :8] = np.random.permutation(np.resize(levels, 8))
        for g in range(8):
            far = levels[np.abs(levels - a[p, g]) >= 10]
            a[p, g + 8] = far[np.random.randint(len(far))]
    return np.exp2(a.ravel()).repeat(32)


def f64(x):
    return np.asarray(x).astype(np.float64)


def striped(idx):
    return np.tile(idx.reshape(-1, 16).T, (8, 1)).astype(np.uint16)


def unstriped(offs):
    return offs[:16].T.reshape(-1).astype(np.int64)


E2M1 = np.array([0.0, 0.5, 1.0, 1.5, 2.0, 3.0, 4.0, 6.0, -0.0, -0.5, -1.0, -1.5, -2.0, -3.0, -4.0, -6.0])


def pack_weight(w, fmt):
    k, n = w.shape
    w = f64(np.asarray(w, np.float32).astype(ml_dtypes.bfloat16)).reshape(k // 32, 32, n)
    amax = np.abs(w).max(1)
    if fmt == "e4m3":
        byte = np.frexp(amax)[1] - 1 + 127 - 7
    else:
        mant, ex = np.frexp(amax / 6.0)
        byte = np.where(mant > 0.5, ex, ex - 1) + 127
    byte = np.clip(np.where(amax > 0, byte, 1), 1, 254)
    scaled = (w * np.exp2(127.0 - byte)[:, None, :]).reshape(k, n).astype(np.float32)
    by_word = np.ascontiguousarray(scaled.reshape(k // 512, 128, 4, n).transpose(0, 1, 3, 2))
    if fmt == "e4m3":
        words = by_word.astype(ml_dtypes.float8_e4m3fn).view(np.uint8)
    else:
        c = by_word.astype(ml_dtypes.float4_e2m1fn).view(np.uint8) & 0xF
        words = (c[..., 0::2] | (c[..., 1::2] << 4)).reshape(k // 512, 128, 2 * n)
    return np.ascontiguousarray(words), np.ascontiguousarray(byte.astype(np.uint8).reshape(k // 512, 16, n))


def unpack_weight(words, scales, fmt):
    g, _, n = scales.shape
    words = np.ascontiguousarray(words).reshape(g, 128, n, -1)
    if fmt == "e4m3":
        vals = words.view(ml_dtypes.float8_e4m3fn).astype(np.float64)
    else:
        nib = np.empty((g, 128, n, 4), np.uint8)
        nib[..., 0::2] = words & 0xF
        nib[..., 1::2] = words >> 4
        vals = E2M1[nib]
    vals = vals * np.repeat(np.exp2(scales.astype(np.float64) - 127.0), 8, axis=1)[..., None]
    return vals.transpose(0, 1, 3, 2).reshape(g * 512, n)


def silu(v):
    return v / (1.0 + np.exp(-np.maximum(v, -700.0)))


K, T, E, C, H, N = 1024, 1024, 8, 256, 512, 128


def by_expert(wq, xq):
    return np.concatenate([wq[e].T @ xq[:, e * C:(e + 1) * C] for e in range(E)], axis=1)


def setup_inputs():
    n = np.random.standard_normal
    s = mx_kscale(K)[:, None]
    u = mx_kscale(H)
    first = np.random.permutation(np.repeat(np.arange(E), T // E))
    second = (first + 1 + np.random.permutation(np.repeat(np.arange(E - 1), -(-T // (E - 1)))[:T])) % E
    while np.bincount(second, minlength=E).max() != T // E:
        load = np.bincount(second, minlength=E); hi, lo = int(load.argmax()), int(load.argmin())
        t = np.flatnonzero((second == hi) & (first != lo))[0]; second[t] = lo
    slot_token = np.empty(E * C, np.int64); pos = np.empty((2, T), np.int64); fill = np.zeros(E, np.int64)
    place = np.stack([np.random.permutation(C) for _ in range(E)])
    for r, deal in enumerate((first, second)):
        for t in np.random.permutation(T):
            e = deal[t]; j = e * C + place[e, fill[e]]; fill[e] += 1; slot_token[j] = t; pos[r, t] = j
    g = np.random.uniform(0.2, 0.8, T)
    x = pack_weight(n((K, T)) * s, "e4m3")
    return {
        "x_words": x[0],
        "x_scales": x[1],
        "w1": (n((E + 1, K, H)) / np.sqrt(K) / s[None] * u[None, None, :]).astype(np.float32),
        "w2": (n((E + 1, H, N)) / np.sqrt(H) / u[None, :, None]).astype(np.float32),
        "gate": np.stack([np.tile(g, (N, 1)), np.tile(1.0 - g, (N, 1))]).astype(np.float32),
        "offs": striped(slot_token),
        "pos1": striped(pos[0]),
        "pos2": striped(pos[1]),
    }


def reference(x_words, x_scales, w1, w2, gate, offs, pos1, pos2):
    idx = unstriped(offs)
    w1q, w2q = mxq(f64(w1), 1, "e4m3"), mxq(f64(w2), 1, "e4m3")
    xs = unpack_weight(x_words, x_scales, "e4m3")
    hs = silu(w1q[E].T @ xs)
    ys = w2q[E].T @ mxq(hs, 0, "e4m3")
    xq = unpack_weight(x_words, x_scales, "e4m3")[:, idx]
    h = silu(by_expert(w1q, xq))
    y = by_expert(w2q, mxq(h, 0, "e4m3"))
    return ys + f64(gate[0]) * y[:, unstriped(pos1)] + f64(gate[1]) * y[:, unstriped(pos2)]

@@ -1,0 +1,273 @@
+from contextlib import ExitStack
+
+import concourse.mybir as mybir
+
+K, T, E, C, H, N = 1024, 1024, 8, 256, 512, 128
+S = E * C
+FLOPS = 2 * (S + T) * (K * H + H * N)
+
+F32 = mybir.dt.float32
+BF16 = mybir.dt.bfloat16
+I32 = mybir.dt.int32
+U32 = mybir.dt.uint32
+U16 = mybir.dt.uint16
+U8 = mybir.dt.uint8
+FP8X4 = mybir.dt.float8_e4m3fn_x4
+SILU = mybir.ActivationFunctionType.Silu
+MULT = mybir.AluOpType.mult
+ADD = mybir.AluOpType.add
+
+P = 128
+PACK = 4
+K_PASS = P * PACK
+PASSES = K // K_PASS
+GROUP = 128
+GATHER = 512
+LIST_ROWS = 16
+SCALAR_M = [[96,96],[96,96],[96,96],[96,96],[96,96],[96,96],[96,96],[96,96],[128,80]]
+LOOKAHEAD = 3
+SLOTS = 12
+SLOT_BYTES = PACK * H * 4
+HALVED = ((0, 0), (E, 1))
+
+
+def tile_moe_shr_mlp_silu_kernel(tc, x_words, x_scales, w1, w2, gate, offs, pos1, pos2, out):
+    nc = tc.nc
+    with ExitStack() as ctx:
+        keep = ctx.enter_context(tc.tile_pool(name="keep", bufs=1))
+        arena = ctx.enter_context(tc.tile_pool(name="arena", bufs=1))
+        ring = ctx.enter_context(tc.tile_pool(name="ring", bufs=3))
+        ps1 = ctx.enter_context(tc.psum_pool(name="ps1", bufs=6))
+        ps2 = ctx.enter_context(tc.psum_pool(name="ps2", bufs=2))
+
+        offs_sb = keep.tile([P, S // LIST_ROWS], U16, name="offs_sb")
+        pos_sb = [keep.tile([P, T // LIST_ROWS], U16, name="pos%d_sb" % r) for r in range(2)]
+        xw = [keep.tile([P, T], I32, name="xw%d" % g, align_bytes=64) for g in range(PASSES)]
+        xs = keep.tile([P, T], U8, name="xs", align_bytes=64)
+        w2_raw = keep.tile([P, E + 1, PACK, N], F32, name="w2_raw")
+        gate_sb = [keep.tile([P, T], F32, name="gate%d" % r) for r in range(2)]
+        y = keep.tile([P, S], F32, name="y")
+        picked = [keep.tile([P, T], F32, name="picked%d" % r) for r in range(2)]
+        routed = keep.tile([P, T], F32, name="routed")
+        result = keep.tile([P, T], F32, name="result")
+        warm = keep.tile([P, 8], F32, name="warm")
+        warm_out = keep.tile([P, 8], F32, name="warm_out")
+
+        nc.vector.memset(xs[:].bitcast(I32), 0)
+        nc.gpsimd.memset(warm[:], 0.0)
+        nc.scalar.activation(warm_out[:], warm[:], SILU)
+
+        w1_raw = {}
+
+        def in_slot(e, g, at, shape, dtype, name):
+            offset = ((e * PASSES + g) % SLOTS) * SLOT_BYTES + at
+            return arena.tile(shape, dtype, name="%s_%d_%d" % (name, e, g), offset=offset, align_bytes=64)
+
+        def load_w1(e, g):
+            raw = in_slot(e, g, 0, [P, PACK, H], F32, "w1_raw")
+            w1_raw[(e, g)] = raw
+            load_w1_columns(e, g, 0, H // 2 if (e, g) in HALVED else H)
+            if (e, g) in HALVED and e > 0:
+                load_w1_columns(e, g, H // 2, H)
+
+        def load_w1_columns(e, g, c0, c1):
+            rows = w1[e, g * K_PASS:(g + 1) * K_PASS, :].rearrange("(p j) c -> p j c", j=PACK)
+            nc.sync.dma_start(out=w1_raw[(e, g)][:, :, c0:c1], in_=rows[:, :, c0:c1])
+
+        def load_w2(e0, e1):
+            nc.sync.dma_start(out=w2_raw[:, e0:e1], in_=w2[e0:e1].rearrange("e (p j) n -> p e j n", j=PACK))
+
+        def load_gate(r):
+            nc.sync.dma_start(out=gate_sb[r][:], in_=gate[r])
+
+        def load_expert(e):
+            if e == E:
+                load_gate(0)
+            elif e % 2 == 0:
+                load_w2(e, e + 2)
+            for g in range(PASSES):
+                load_w1(e, g)
+            if e == E:
+                load_gate(1)
+                load_w2(E, E + 1)
+
+        load_w1(0, 0)
+        nc.sync.dma_start(offs_sb[:], offs)
+        nc.sync.dma_start(out=xw[0][:], in_=x_words[0].rearrange("p t r -> p (t r)").bitcast(I32))
+        load_w1_columns(0, 0, H // 2, H)
+        nc.sync.dma_start(out=xw[1][:], in_=x_words[1].rearrange("p t r -> p (t r)").bitcast(I32))
+        for q in range(4):
+            nc.sync.dma_start(out=xs[32 * q:32 * q + 4 * PASSES, :].bitcast(I32), in_=x_scales[:, 4 * q:4 * q + 4, :].bitcast(I32))
+        load_w1(0, 1)
+        load_w2(0, 2)
+        nc.sync.dma_start(pos_sb[0][:], pos1)
+        nc.sync.dma_start(pos_sb[1][:], pos2)
+        for e in range(1, LOOKAHEAD):
+            load_expert(e)
+
+        slots = {}
+        w1_q = {}
+        w1_bf = {}
+        w2_bf = {}
+        w2_q = {}
+        h_bf = {}
+        h_q = {}
+        first_bank = {}
+
+        def gather_tokens(e):
+            lst = offs_sb[:, e * C // LIST_ROWS:(e + 1) * C // LIST_ROWS]
+            if e < 2:
+                gw = [keep.tile([P, C], U32, name="gw%d_%d" % (g, e), align_bytes=64) for g in range(PASSES)]
+                gs = keep.tile([P, C], U8, name="gs_%d" % e, align_bytes=64)
+            else:
+                gw = [in_slot(e - 2, 1, 2048 + 1024 * g, [P, C], U32, "gw%d" % g) for g in range(PASSES)]
+                gs = in_slot(e - 2, 1, 4096, [P, C], U8, "gs")
+            for g in range(PASSES):
+                nc.vector.tensor_copy(gw[g][:], xw[g][:].bitcast(U32).indirect(lst))
+            nc.vector.tensor_copy(gs[:], xs[:].indirect(lst))
+            slots[e] = (gw, gs)
+
+        def round_w1(e, g):
+            rounded = ring.tile([P, H * PACK], BF16, name="w1_bf", align_bytes=64, bufs=3)
+            dst = rounded[:].rearrange("p (t m j) -> p m j t", t=PACK, j=PACK)
+            src = w1_raw[(e, g)][:].rearrange("p j (m t) -> p m j t", t=PACK)
+            ms = SCALAR_M[e][g]
+            cuts = [0, P // 2, ms] if (e, g) in HALVED and ms > P // 2 else [0, ms]
+            for m0, m1 in zip(cuts, cuts[1:]):
+                nc.scalar.copy(dst[:, m0:m1], src[:, m0:m1])
+            if ms < P:
+                nc.vector.tensor_copy(dst[:, ms:], src[:, ms:])
+            w1_bf[(e, g)] = rounded
+
+        def quantise_w1(e, g):
+            if g == 0:
+                w1_q[e] = (ring.tile([P, PASSES, H], U32, name="w1_codes", align_bytes=64),
+                           ring.tile([P, PASSES, H], U8, name="w1_scales", align_bytes=64))
+            codes, scales = w1_q[e]
+            nc.vector.quantize_mx(out=codes[:, g, :].bitcast(FP8X4), scales=scales[:, g, :], in_=w1_bf[(e, g)][:])
+
+        def round_w2(e, slot):
+            rounded = in_slot(slot[0], slot[1], 6144, [P, N * PACK], BF16, "w2_bf")
+            dst = rounded[:].rearrange("p (c i j) -> p c j i", i=4, j=PACK)
+            src = w2_raw[:, e].rearrange("p j (c i) -> p c j i", i=4)
+            nc.vector.tensor_copy(dst, src)
+            w2_bf[e] = rounded
+
+        def quantise_w2(e):
+            codes = ring.tile([P, N], U32, name="w2_codes", align_bytes=64)
+            scales = ring.tile([P, N], U8, name="w2_scales", align_bytes=64)
+            nc.vector.quantize_mx(out=codes[:].bitcast(FP8X4), scales=scales[:], in_=w2_bf[e][:])
+            w2_q[e] = (codes, scales)
+
+        def first_layer(e, words, planes, c0, h):
+            w_codes, w_scales = w1_q[e]
+            for u in range(C // GROUP):
+                cols = slice(c0 + u * GROUP, c0 + (u + 1) * GROUP)
+                acc = ps1.tile([P, PACK, GROUP], F32, name="acc1")
+                if u == 0:
+                    first_bank[e] = acc
+                if e == E:
+                    order = [(g, t, g == 0 and t == 0, g == PASSES - 1 and t == PACK - 1) for g in range(PASSES) for t in range(PACK)]
+                else:
+                    order = [(g, t, g == 0, g == PASSES - 1) for t in range(PACK) for g in range(PASSES)]
+                for g, t, first, last in order:
+                    ch = slice(t * P, (t + 1) * P)
+                    nc.tensor.matmul_mx(
+                        out=acc[:, t, :],
+                        lhsT=w_codes[:, g, ch].bitcast(FP8X4), lhsT_scale=w_scales[:, g, ch],
+                        rhs=words[g][:, cols].bitcast(FP8X4), rhs_scale=planes[4 * g:, cols],
+                        start=first, stop=last,
+                    )
+                nc.scalar.activation(
+                    h[:, u * GROUP * PACK:(u + 1) * GROUP * PACK].rearrange("p (n t) -> p n t", t=PACK),
+                    acc[:].rearrange("p t n -> p n t"), SILU)
+
+        def quantise_h(h, slot):
+            if slot is None:
+                codes = ring.tile([P, C], U32, name="h_codes", align_bytes=64)
+                scales = ring.tile([P, C], U8, name="h_scales", align_bytes=64)
+            else:
+                codes = in_slot(slot[0], slot[1], 0, [P, C], U32, "h_codes")
+                scales = in_slot(slot[0], slot[1], 1024, [P, C], U8, "h_scales")
+            nc.vector.quantize_mx(out=codes[:].bitcast(FP8X4), scales=scales[:], in_=h[:])
+            return codes, scales
+
+        def second_layer(e, h_codes, h_scales, acc):
+            w_codes, w_scales = w2_q[e]
+            nc.tensor.matmul_mx(out=acc, lhsT=w_codes[:].bitcast(FP8X4), lhsT_scale=w_scales[:],
+                                rhs=h_codes[:].bitcast(FP8X4), rhs_scale=h_scales[:], start=True, stop=True)
+
+        def routed_first(e):
+            if e < E - 1:
+                h = in_slot(e + 1, 1, 0, [P, C * PACK], BF16, "h_bf")
+            else:
+                h = ring.tile([P, C * PACK], BF16, name="h_bf", align_bytes=64)
+            first_layer(e, slots[e][0], slots[e][1], 0, h)
+            h_bf[e] = h
+
+        def routed_second(e):
+            if e < E - 1:
+                acc = first_bank[e + 1][:].rearrange("p t n -> p (t n)")[:, :C]
+            else:
+                bank = ps2.tile([P, C], F32, name="acc2")
+                acc = bank[:]
+            second_layer(e, h_q[e][0], h_q[e][1], acc)
+            nc.scalar.copy(y[:, e * C:(e + 1) * C], acc)
+
+        def pick(r, t0):
+            cols = slice(t0, t0 + GATHER)
+            lst = pos_sb[r][:, t0 // LIST_ROWS:(t0 + GATHER) // LIST_ROWS]
+            nc.vector.tensor_tensor(picked[r][:, cols], y[:].indirect(lst), gate_sb[r][:, cols], MULT)
+
+        gather_tokens(0)
+        gather_tokens(1)
+        for e in range(E):
+            if e + LOOKAHEAD <= E:
+                load_expert(e + LOOKAHEAD)
+            round_w1(e, 0)
+            if e >= 1:
+                round_w2(e - 1, (e, 0))
+            if e >= 2:
+                h_q[e - 2] = quantise_h(h_bf[e - 2], (e, 0))
+            quantise_w1(e, 0)
+            if e >= 1:
+                quantise_w2(e - 1)
+            round_w1(e, 1)
+            if e == E - 1:
+                round_w2(e, (e, 1))
+            quantise_w1(e, 1)
+            if e == E - 1:
+                quantise_w2(e)
+            if e >= 1:
+                routed_first(e - 1)
+            if e >= 2:
+                routed_second(e - 2)
+            if e + 2 < E:
+                gather_tokens(e + 2)
+
+        h_q[E - 2] = quantise_h(h_bf[E - 2], None)
+        routed_first(E - 1)
+        routed_second(E - 2)
+        h_q[E - 1] = quantise_h(h_bf[E - 1], None)
+        routed_second(E - 1)
+        for g in range(PASSES):
+            round_w1(E, g)
+            quantise_w1(E, g)
+        round_w2(E, (E, 1))
+        quantise_w2(E)
+
+        for c in range(T // C):
+            t0 = c * C
+            cols = slice(t0, t0 + C)
+            h = ring.tile([P, C * PACK], BF16, name="h_bf", align_bytes=64)
+            first_layer(E, xw, xs, t0, h)
+            h_codes, h_scales = quantise_h(h, None)
+            if t0 % GATHER == 0:
+                wide = slice(t0, t0 + GATHER)
+                pick(0, t0)
+                pick(1, t0)
+                nc.vector.tensor_tensor(routed[:, wide], picked[0][:, wide], picked[1][:, wide], ADD)
+            bank = ps2.tile([P, C], F32, name="acc2")
+            second_layer(E, h_codes, h_scales, bank[:])
+            nc.vector.tensor_tensor(result[:, cols], bank[:], routed[:, cols], ADD)
+            nc.sync.dma_start(out=out[:, cols], in_=result[:, cols])

@@ -22,13 +22,24 @@ PACK = 4
 K_PASS = P * PACK
 PASSES = K // K_PASS
 GROUP = 128
-GATHER = 512
 LIST_ROWS = 16
-SCALAR_M = [[96,96],[96,96],[96,96],[96,96],[96,96],[96,96],[96,96],[96,96],[128,80]]
-LOOKAHEAD = 3
-SLOTS = 12
-SLOT_BYTES = PACK * H * 4
-HALVED = ((0, 0), (E, 1))
+ORDER = [0, 1, 2, 3, 4, 5, 6, 7, 8]
+SCALAR_M = [[128, 128], [80, 32], [80, 32], [80, 32], [80, 32], [80, 32], [64, 32], [32, 80], [64, 80]]
+WHOLE = [1, 2, 3, 4, 5, 6]
+H_AFTER = [(1, 1), (2, 1), (3, 1), (4, 1), (5, 1), (6, 1), (7, 1), None, None, None, None, None]
+Q_AFTER = [(2, 0), (3, 0), (4, 0), (5, 0), (4, 0), (5, 0), (6, 0), (7, 0), (1, 0), (2, 0), (3, 0), (4, 0)]
+GATHER_AFTER = [None, None, None, None, (0, 0), (1, 0), (2, 0), (3, 0)]
+W2_AFTER = [(0, 0), (1, 0), (2, 0), (3, 0), (7, 0), (7, 0), (7, 0), (7, 0), (7, 1)]
+W2_SCALAR = [1, 1, 1, 1, 0, 0, 0, 0, 0]
+ONE = [0, 1, 2, 3, 4, 5, 6, 7, 8]
+PS1 = 5
+LOADS = ['o', 'x0', 'x1', 'w00', 's', 'w01', 'v02', 'w10', 'w11', 'v24', 'w20', 'w21', 'w30', 'w31', 'w40', 'w41', 'w50', 'w51', 'w60', 'w61', 'w70', 'w71', 'p', 'v46', 'v68', 'v89', 'w80', 'g0a', 'w81', 'g1a', 'g0b', 'g1b']
+PICK0 = 2
+LAST = [0, 1, 2, 3]
+PASS_BYTES = PACK * H * 4
+SLOT_BYTES = PASSES * PASS_BYTES
+STAGES = 4
+STAGE_BYTES = PACK * H * 2
 
 
 def tile_moe_shr_mlp_silu_kernel(tc, x_words, x_scales, w1, w2, gate, offs, pos1, pos2, out):
@@ -37,8 +48,8 @@ def tile_moe_shr_mlp_silu_kernel(tc, x_words, x_scales, w1, w2, gate, offs, pos1
         keep = ctx.enter_context(tc.tile_pool(name="keep", bufs=1))
         arena = ctx.enter_context(tc.tile_pool(name="arena", bufs=1))
         ring = ctx.enter_context(tc.tile_pool(name="ring", bufs=3))
-        ps1 = ctx.enter_context(tc.psum_pool(name="ps1", bufs=6))
-        ps2 = ctx.enter_context(tc.psum_pool(name="ps2", bufs=2))
+        ps1 = ctx.enter_context(tc.psum_pool(name="ps1", bufs=PS1))
+        ps2 = ctx.enter_context(tc.psum_pool(name="ps2", bufs=8 - PS1))
 
         offs_sb = keep.tile([P, S // LIST_ROWS], U16, name="offs_sb")
         pos_sb = [keep.tile([P, T // LIST_ROWS], U16, name="pos%d_sb" % r) for r in range(2)]
@@ -47,9 +58,6 @@ def tile_moe_shr_mlp_silu_kernel(tc, x_words, x_scales, w1, w2, gate, offs, pos1
         w2_raw = keep.tile([P, E + 1, PACK, N], F32, name="w2_raw")
         gate_sb = [keep.tile([P, T], F32, name="gate%d" % r) for r in range(2)]
         y = keep.tile([P, S], F32, name="y")
-        picked = [keep.tile([P, T], F32, name="picked%d" % r) for r in range(2)]
-        routed = keep.tile([P, T], F32, name="routed")
-        result = keep.tile([P, T], F32, name="result")
         warm = keep.tile([P, 8], F32, name="warm")
         warm_out = keep.tile([P, 8], F32, name="warm_out")
 
@@ -57,22 +65,43 @@ def tile_moe_shr_mlp_silu_kernel(tc, x_words, x_scales, w1, w2, gate, offs, pos1
         nc.gpsimd.memset(warm[:], 0.0)
         nc.scalar.activation(warm_out[:], warm[:], SILU)
 
+        def placed(offset, shape, dtype, name):
+            return arena.tile(shape, dtype, name=name, offset=offset, align_bytes=64)
+
+        def slot_at(s, g=0):
+            return s * SLOT_BYTES + g * PASS_BYTES
+
+        def stage_at(s, g):
+            return (E + 1) * SLOT_BYTES + ((s * PASSES + g) % STAGES) * STAGE_BYTES
+
+        used = {}
+        w2_at = {}
+
+        def after(where, shape, dtype, size, name):
+            if where is None:
+                return keep.tile(shape, dtype, name=name, align_bytes=64)
+            if where[0] == "w":
+                return placed(w2_at[where[1]], shape, dtype, name)
+            at = used.get(where, 0)
+            if name.startswith("w2_bf"):
+                w2_at[int(name[-1])] = slot_at(where[0], where[1]) + at
+            used[where] = at + shape[1] * size
+            assert used[where] <= PASS_BYTES
+            return placed(slot_at(where[0], where[1]) + at, shape, dtype, name)
+
         w1_raw = {}
 
-        def in_slot(e, g, at, shape, dtype, name):
-            offset = ((e * PASSES + g) % SLOTS) * SLOT_BYTES + at
-            return arena.tile(shape, dtype, name="%s_%d_%d" % (name, e, g), offset=offset, align_bytes=64)
+        def load_w1_pass(s, g):
+            raw = placed(slot_at(s, g), [P, PACK, H], F32, "w1_raw_%d_%d" % (s, g))
+            rows = w1[ORDER[s], g * K_PASS:(g + 1) * K_PASS, :]
+            nc.sync.dma_start(out=raw[:], in_=rows.rearrange("(p j) c -> p j c", j=PACK))
+            w1_raw[(s, g)] = raw[:]
 
-        def load_w1(e, g):
-            raw = in_slot(e, g, 0, [P, PACK, H], F32, "w1_raw")
-            w1_raw[(e, g)] = raw
-            load_w1_columns(e, g, 0, H // 2 if (e, g) in HALVED else H)
-            if (e, g) in HALVED and e > 0:
-                load_w1_columns(e, g, H // 2, H)
-
-        def load_w1_columns(e, g, c0, c1):
-            rows = w1[e, g * K_PASS:(g + 1) * K_PASS, :].rearrange("(p j) c -> p j c", j=PACK)
-            nc.sync.dma_start(out=w1_raw[(e, g)][:, :, c0:c1], in_=rows[:, :, c0:c1])
+        def load_w1(s):
+            raw = placed(slot_at(s), [P, PASSES, PACK, H], F32, "w1_raw_%d" % s)
+            nc.sync.dma_start(out=raw[:], in_=w1[ORDER[s]].rearrange("(g p j) c -> p g j c", g=PASSES, j=PACK))
+            for g in range(PASSES):
+                w1_raw[(s, g)] = raw[:, g]
 
         def load_w2(e0, e1):
             nc.sync.dma_start(out=w2_raw[:, e0:e1], in_=w2[e0:e1].rearrange("e (p j) n -> p e j n", j=PACK))
@@ -80,30 +109,36 @@ def tile_moe_shr_mlp_silu_kernel(tc, x_words, x_scales, w1, w2, gate, offs, pos1
         def load_gate(r):
             nc.sync.dma_start(out=gate_sb[r][:], in_=gate[r])
 
-        def load_expert(e):
-            if e == E:
-                load_gate(0)
-            elif e % 2 == 0:
-                load_w2(e, e + 2)
-            for g in range(PASSES):
-                load_w1(e, g)
-            if e == E:
-                load_gate(1)
-                load_w2(E, E + 1)
+        def load_x(g):
+            nc.sync.dma_start(out=xw[g][:], in_=x_words[g].rearrange("p t r -> p (t r)").bitcast(I32))
 
-        load_w1(0, 0)
-        nc.sync.dma_start(offs_sb[:], offs)
-        nc.sync.dma_start(out=xw[0][:], in_=x_words[0].rearrange("p t r -> p (t r)").bitcast(I32))
-        load_w1_columns(0, 0, H // 2, H)
-        nc.sync.dma_start(out=xw[1][:], in_=x_words[1].rearrange("p t r -> p (t r)").bitcast(I32))
-        for q in range(4):
-            nc.sync.dma_start(out=xs[32 * q:32 * q + 4 * PASSES, :].bitcast(I32), in_=x_scales[:, 4 * q:4 * q + 4, :].bitcast(I32))
-        load_w1(0, 1)
-        load_w2(0, 2)
-        nc.sync.dma_start(pos_sb[0][:], pos1)
-        nc.sync.dma_start(pos_sb[1][:], pos2)
-        for e in range(1, LOOKAHEAD):
-            load_expert(e)
+        def load_scales():
+            for q in range(4):
+                nc.sync.dma_start(out=xs[32 * q:32 * q + 4 * PASSES, :].bitcast(I32), in_=x_scales[:, 4 * q:4 * q + 4, :].bitcast(I32))
+
+        def load_pos():
+            nc.sync.dma_start(pos_sb[0][:], pos1)
+            nc.sync.dma_start(pos_sb[1][:], pos2)
+
+        for name in LOADS:
+            if name == "o":
+                nc.sync.dma_start(offs_sb[:], offs)
+            elif name == "s":
+                load_scales()
+            elif name == "p":
+                load_pos()
+            elif name[0] == "x":
+                load_x(int(name[1]))
+            elif name[0] == "g":
+                half = {"": slice(0, T), "a": slice(0, T // 2), "b": slice(T // 2, T)}[name[2:]]
+                nc.sync.dma_start(out=gate_sb[int(name[1])][:, half], in_=gate[int(name[1])][:, half])
+            elif name[0] == "v":
+                load_w2(int(name[1]), int(name[2]))
+            elif int(name[1]) in WHOLE:
+                if name[2] == "1":
+                    load_w1(int(name[1]))
+            else:
+                load_w1_pass(int(name[1]), int(name[2]))
 
         slots = {}
         w1_q = {}
@@ -112,50 +147,44 @@ def tile_moe_shr_mlp_silu_kernel(tc, x_words, x_scales, w1, w2, gate, offs, pos1
         w2_q = {}
         h_bf = {}
         h_q = {}
-        first_bank = {}
 
         def gather_tokens(e):
             lst = offs_sb[:, e * C // LIST_ROWS:(e + 1) * C // LIST_ROWS]
-            if e < 2:
-                gw = [keep.tile([P, C], U32, name="gw%d_%d" % (g, e), align_bytes=64) for g in range(PASSES)]
-                gs = keep.tile([P, C], U8, name="gs_%d" % e, align_bytes=64)
-            else:
-                gw = [in_slot(e - 2, 1, 2048 + 1024 * g, [P, C], U32, "gw%d" % g) for g in range(PASSES)]
-                gs = in_slot(e - 2, 1, 4096, [P, C], U8, "gs")
+            gw = [after(GATHER_AFTER[e], [P, C], U32, 4, "gw%d_%d" % (g, e)) for g in range(PASSES)]
+            gs = after(GATHER_AFTER[e], [P, C], U8, 1, "gs_%d" % e)
             for g in range(PASSES):
                 nc.vector.tensor_copy(gw[g][:], xw[g][:].bitcast(U32).indirect(lst))
             nc.vector.tensor_copy(gs[:], xs[:].indirect(lst))
             slots[e] = (gw, gs)
 
         def round_w1(e, g):
-            rounded = ring.tile([P, H * PACK], BF16, name="w1_bf", align_bytes=64, bufs=3)
-            dst = rounded[:].rearrange("p (t m j) -> p m j t", t=PACK, j=PACK)
-            src = w1_raw[(e, g)][:].rearrange("p j (m t) -> p m j t", t=PACK)
+            rounded = placed(stage_at(e, g), [P, H * PACK], BF16, "w1_bf_%d_%d" % (e, g))
+            dst = rounded[:].rearrange("p (t m a b) -> p m a t b", t=PACK, a=2, b=2)
+            src = w1_raw[(e, g)].rearrange("p (a b) (m t) -> p m a t b", t=PACK, b=2)
             ms = SCALAR_M[e][g]
-            cuts = [0, P // 2, ms] if (e, g) in HALVED and ms > P // 2 else [0, ms]
-            for m0, m1 in zip(cuts, cuts[1:]):
-                nc.scalar.copy(dst[:, m0:m1], src[:, m0:m1])
+            if ms > 0:
+                nc.scalar.copy(dst[:, :ms], src[:, :ms])
             if ms < P:
                 nc.vector.tensor_copy(dst[:, ms:], src[:, ms:])
             w1_bf[(e, g)] = rounded
 
         def quantise_w1(e, g):
             if g == 0:
-                w1_q[e] = (ring.tile([P, PASSES, H], U32, name="w1_codes", align_bytes=64),
-                           ring.tile([P, PASSES, H], U8, name="w1_scales", align_bytes=64))
+                w1_q[e] = (ring.tile([P, PASSES, H], U32, name="w1_codes", align_bytes=64, bufs=2),
+                           ring.tile([P, PASSES, H], U8, name="w1_scales", align_bytes=64, bufs=2))
             codes, scales = w1_q[e]
             nc.vector.quantize_mx(out=codes[:, g, :].bitcast(FP8X4), scales=scales[:, g, :], in_=w1_bf[(e, g)][:])
 
-        def round_w2(e, slot):
-            rounded = in_slot(slot[0], slot[1], 6144, [P, N * PACK], BF16, "w2_bf")
-            dst = rounded[:].rearrange("p (c i j) -> p c j i", i=4, j=PACK)
-            src = w2_raw[:, e].rearrange("p j (c i) -> p c j i", i=4)
-            nc.vector.tensor_copy(dst, src)
+        def round_w2(e):
+            rounded = after(W2_AFTER[e], [P, N * PACK], BF16, 2, "w2_bf_%d" % e)
+            dst = rounded[:].rearrange("p (c i a b) -> p c a i b", i=4, a=2, b=2)
+            src = w2_raw[:, e].rearrange("p (a b) (c i) -> p c a i b", i=4, b=2)
+            (nc.scalar.copy if W2_SCALAR[e] else nc.vector.tensor_copy)(dst, src)
             w2_bf[e] = rounded
 
         def quantise_w2(e):
-            codes = ring.tile([P, N], U32, name="w2_codes", align_bytes=64)
-            scales = ring.tile([P, N], U8, name="w2_scales", align_bytes=64)
+            codes = keep.tile([P, N], U32, name="w2_codes_%d" % e, align_bytes=64)
+            scales = keep.tile([P, N], U8, name="w2_scales_%d" % e, align_bytes=64)
             nc.vector.quantize_mx(out=codes[:].bitcast(FP8X4), scales=scales[:], in_=w2_bf[e][:])
             w2_q[e] = (codes, scales)
 
@@ -164,9 +193,7 @@ def tile_moe_shr_mlp_silu_kernel(tc, x_words, x_scales, w1, w2, gate, offs, pos1
             for u in range(C // GROUP):
                 cols = slice(c0 + u * GROUP, c0 + (u + 1) * GROUP)
                 acc = ps1.tile([P, PACK, GROUP], F32, name="acc1")
-                if u == 0:
-                    first_bank[e] = acc
-                if e == E:
+                if e in ONE:
                     order = [(g, t, g == 0 and t == 0, g == PASSES - 1 and t == PACK - 1) for g in range(PASSES) for t in range(PACK)]
                 else:
                     order = [(g, t, g == 0, g == PASSES - 1) for t in range(PACK) for g in range(PASSES)]
@@ -182,92 +209,106 @@ def tile_moe_shr_mlp_silu_kernel(tc, x_words, x_scales, w1, w2, gate, offs, pos1
                     h[:, u * GROUP * PACK:(u + 1) * GROUP * PACK].rearrange("p (n t) -> p n t", t=PACK),
                     acc[:].rearrange("p t n -> p n t"), SILU)
 
-        def quantise_h(h, slot):
-            if slot is None:
-                codes = ring.tile([P, C], U32, name="h_codes", align_bytes=64)
-                scales = ring.tile([P, C], U8, name="h_scales", align_bytes=64)
-            else:
-                codes = in_slot(slot[0], slot[1], 0, [P, C], U32, "h_codes")
-                scales = in_slot(slot[0], slot[1], 1024, [P, C], U8, "h_scales")
+        def quantise_h(h, where, name):
+            codes = after(where, [P, C], U32, 4, "h_codes_" + name)
+            scales = after(where, [P, C], U8, 1, "h_scales_" + name)
             nc.vector.quantize_mx(out=codes[:].bitcast(FP8X4), scales=scales[:], in_=h[:])
             return codes, scales
 
-        def second_layer(e, h_codes, h_scales, acc):
+        def second_layer(e, h_codes, h_scales):
             w_codes, w_scales = w2_q[e]
-            nc.tensor.matmul_mx(out=acc, lhsT=w_codes[:].bitcast(FP8X4), lhsT_scale=w_scales[:],
+            acc = ps2.tile([P, C], F32, name="acc2")
+            nc.tensor.matmul_mx(out=acc[:], lhsT=w_codes[:].bitcast(FP8X4), lhsT_scale=w_scales[:],
                                 rhs=h_codes[:].bitcast(FP8X4), rhs_scale=h_scales[:], start=True, stop=True)
+            return acc
 
-        def routed_first(e):
-            if e < E - 1:
-                h = in_slot(e + 1, 1, 0, [P, C * PACK], BF16, "h_bf")
-            else:
-                h = ring.tile([P, C * PACK], BF16, name="h_bf", align_bytes=64)
-            first_layer(e, slots[e][0], slots[e][1], 0, h)
-            h_bf[e] = h
+        sh = ORDER.index(E)
+        units = [(ORDER.index(e), e, 0) for e in range(E)] + [(sh, E, c) for c in range(T // C)]
+        todo = []
+        for u, (s, e, c) in enumerate(units):
+            todo.append(("first", u))
+            todo.append(("hq", u))
+            if e < E:
+                todo.append(("second", u))
+        todo = sorted(todo, key=lambda x: (units[x[1]][0], x[1]))
+        w2_todo = list(range(E + 1))
+        g_todo = list(range(E))
 
-        def routed_second(e):
-            if e < E - 1:
-                acc = first_bank[e + 1][:].rearrange("p t n -> p (t n)")[:, :C]
-            else:
-                bank = ps2.tile([P, C], F32, name="acc2")
-                acc = bank[:]
-            second_layer(e, h_q[e][0], h_q[e][1], acc)
-            nc.scalar.copy(y[:, e * C:(e + 1) * C], acc)
+        def emit(now):
+            rounded = []
+            again = True
+            while again:
+                again = False
+                for item in list(todo):
+                    kind, u = item
+                    s, e, c = units[u]
+                    if kind == "first":
+                        w = H_AFTER[u]
+                        if (s, 1) <= now and (w is None or (w[1] in w2_q if w[0] == "w" else w <= now)) and (e == E or e in slots):
+                            if w is None:
+                                h = ring.tile([P, C * PACK], BF16, name="h_bf", align_bytes=64)
+                            else:
+                                h = after(w, [P, C * PACK], BF16, 2, "h_bf_%d" % u)
+                            if e < E:
+                                first_layer(s, slots[e][0], slots[e][1], 0, h)
+                            else:
+                                first_layer(s, xw, xs, c * C, h)
+                            h_bf[u] = h
+                            todo.remove(item)
+                            again = True
+                    elif kind == "hq":
+                        w = Q_AFTER[u]
+                        if u in h_bf and w <= now:
+                            h_q[u] = quantise_h(h_bf[u], w, "%d" % u)
+                            todo.remove(item)
+                            again = True
+                    elif u in h_q and e in w2_q:
+                        acc = second_layer(e, h_q[u][0], h_q[u][1])
+                        nc.scalar.copy(y[:, e * C:(e + 1) * C], acc[:])
+                        todo.remove(item)
+                        again = True
+                for e in list(w2_todo):
+                    if W2_AFTER[e] <= now:
+                        round_w2(e)
+                        rounded.append(e)
+                        w2_todo.remove(e)
+                for e in list(g_todo):
+                    if GATHER_AFTER[e] is None or GATHER_AFTER[e] <= now:
+                        gather_tokens(e)
+                        g_todo.remove(e)
+                        again = True
+                for e in rounded:
+                    quantise_w2(e)
+                    again = True
+                rounded = []
 
-        def pick(r, t0):
-            cols = slice(t0, t0 + GATHER)
-            lst = pos_sb[r][:, t0 // LIST_ROWS:(t0 + GATHER) // LIST_ROWS]
-            nc.vector.tensor_tensor(picked[r][:, cols], y[:].indirect(lst), gate_sb[r][:, cols], MULT)
+        emit((-1, 0))
+        for s in range(E + 1):
+            round_w1(s, 0)
+            round_w1(s, 1)
+            quantise_w1(s, 0)
+            emit((s, 0))
+            quantise_w1(s, 1)
+            emit((s, 1))
+        assert not todo and not w2_todo and not g_todo
 
-        gather_tokens(0)
-        gather_tokens(1)
-        for e in range(E):
-            if e + LOOKAHEAD <= E:
-                load_expert(e + LOOKAHEAD)
-            round_w1(e, 0)
-            if e >= 1:
-                round_w2(e - 1, (e, 0))
-            if e >= 2:
-                h_q[e - 2] = quantise_h(h_bf[e - 2], (e, 0))
-            quantise_w1(e, 0)
-            if e >= 1:
-                quantise_w2(e - 1)
-            round_w1(e, 1)
-            if e == E - 1:
-                round_w2(e, (e, 1))
-            quantise_w1(e, 1)
-            if e == E - 1:
-                quantise_w2(e)
-            if e >= 1:
-                routed_first(e - 1)
-            if e >= 2:
-                routed_second(e - 2)
-            if e + 2 < E:
-                gather_tokens(e + 2)
+        picked = [placed(slot_at(5, r), [P, T], F32, "picked%d" % r) for r in range(2)]
+        partial = placed(slot_at(5, 0) + 4096, [P, T], F32, "partial")
+        result = placed(slot_at(5, 1) + 4096, [P, T], F32, "result")
 
-        h_q[E - 2] = quantise_h(h_bf[E - 2], None)
-        routed_first(E - 1)
-        routed_second(E - 2)
-        h_q[E - 1] = quantise_h(h_bf[E - 1], None)
-        routed_second(E - 1)
-        for g in range(PASSES):
-            round_w1(E, g)
-            quantise_w1(E, g)
-        round_w2(E, (E, 1))
-        quantise_w2(E)
+        def pick(r, c0, c1):
+            cols = slice(c0, c1)
+            nc.vector.tensor_tensor(picked[r][:, cols], y[:].indirect(pos_sb[r][:, c0 // LIST_ROWS:c1 // LIST_ROWS]), gate_sb[r][:, cols], MULT)
 
         for c in range(T // C):
-            t0 = c * C
-            cols = slice(t0, t0 + C)
-            h = ring.tile([P, C * PACK], BF16, name="h_bf", align_bytes=64)
-            first_layer(E, xw, xs, t0, h)
-            h_codes, h_scales = quantise_h(h, None)
-            if t0 % GATHER == 0:
-                wide = slice(t0, t0 + GATHER)
-                pick(0, t0)
-                pick(1, t0)
-                nc.vector.tensor_tensor(routed[:, wide], picked[0][:, wide], picked[1][:, wide], ADD)
-            bank = ps2.tile([P, C], F32, name="acc2")
-            second_layer(E, h_codes, h_scales, bank[:])
-            nc.vector.tensor_tensor(result[:, cols], bank[:], routed[:, cols], ADD)
-            nc.sync.dma_start(out=out[:, cols], in_=result[:, cols])
+            cols = slice(c * C, (c + 1) * C)
+            if c % PICK0 == 0:
+                wide = slice(c * C, (c + PICK0) * C)
+                pick(0, wide.start, wide.stop)
+                pick(1, wide.start, wide.stop)
+                nc.vector.tensor_tensor(partial[:, wide], picked[0][:, wide], picked[1][:, wide], ADD)
+            acc = second_layer(E, h_q[E + c][0], h_q[E + c][1])
+            nc.vector.tensor_tensor(result[:, cols], acc[:], partial[:, cols], ADD)
+            if c in LAST:
+                first = (max([x for x in LAST if x < c] + [-1]) + 1) * C
+                nc.sync.dma_start(out=out[:, first:cols.stop], in_=result[:, first:cols.stop])

from contextlib import ExitStack

import concourse.mybir as mybir

K, T, E, C, H, N = 1024, 1024, 8, 256, 512, 128
S = E * C
FLOPS = 2 * (S + T) * (K * H + H * N)

F32 = mybir.dt.float32
BF16 = mybir.dt.bfloat16
I32 = mybir.dt.int32
U32 = mybir.dt.uint32
U16 = mybir.dt.uint16
U8 = mybir.dt.uint8
FP8X4 = mybir.dt.float8_e4m3fn_x4
SILU = mybir.ActivationFunctionType.Silu
MULT = mybir.AluOpType.mult
ADD = mybir.AluOpType.add

P = 128
PACK = 4
K_PASS = P * PACK
PASSES = K // K_PASS
GROUP = 128
LIST_ROWS = 16
ORDER = [0, 1, 2, 3, 4, 5, 6, 7, 8]
SCALAR_M = [[128, 128], [80, 32], [80, 32], [80, 32], [80, 32], [80, 32], [64, 32], [32, 80], [64, 80]]
WHOLE = [1, 2, 3, 4, 5, 6]
H_AFTER = [(1, 1), (2, 1), (3, 1), (4, 1), (5, 1), (6, 1), (7, 1), None, None, None, None, None]
Q_AFTER = [(2, 0), (3, 0), (4, 0), (5, 0), (4, 0), (5, 0), (6, 0), (7, 0), (1, 0), (2, 0), (3, 0), (4, 0)]
GATHER_AFTER = [None, None, None, None, (0, 0), (1, 0), (2, 0), (3, 0)]
W2_AFTER = [(0, 0), (1, 0), (2, 0), (3, 0), (7, 0), (7, 0), (7, 0), (7, 0), (7, 1)]
W2_SCALAR = [1, 1, 1, 1, 0, 0, 0, 0, 0]
ONE = [0, 1, 2, 3, 4, 5, 6, 7, 8]
PS1 = 5
LOADS = ['o', 'x0', 'x1', 'w00', 's', 'w01', 'v02', 'w10', 'w11', 'v24', 'w20', 'w21', 'w30', 'w31', 'w40', 'w41', 'w50', 'w51', 'w60', 'w61', 'w70', 'w71', 'p', 'v46', 'v68', 'v89', 'w80', 'g0a', 'w81', 'g1a', 'g0b', 'g1b']
PICK0 = 2
LAST = [0, 1, 2, 3]
PASS_BYTES = PACK * H * 4
SLOT_BYTES = PASSES * PASS_BYTES
STAGES = 4
STAGE_BYTES = PACK * H * 2


def tile_moe_shr_mlp_silu_kernel(tc, x_words, x_scales, w1, w2, gate, offs, pos1, pos2, out):
    nc = tc.nc
    with ExitStack() as ctx:
        keep = ctx.enter_context(tc.tile_pool(name="keep", bufs=1))
        arena = ctx.enter_context(tc.tile_pool(name="arena", bufs=1))
        ring = ctx.enter_context(tc.tile_pool(name="ring", bufs=3))
        ps1 = ctx.enter_context(tc.psum_pool(name="ps1", bufs=PS1))
        ps2 = ctx.enter_context(tc.psum_pool(name="ps2", bufs=8 - PS1))

        offs_sb = keep.tile([P, S // LIST_ROWS], U16, name="offs_sb")
        pos_sb = [keep.tile([P, T // LIST_ROWS], U16, name="pos%d_sb" % r) for r in range(2)]
        xw = [keep.tile([P, T], I32, name="xw%d" % g, align_bytes=64) for g in range(PASSES)]
        xs = keep.tile([P, T], U8, name="xs", align_bytes=64)
        w2_raw = keep.tile([P, E + 1, PACK, N], F32, name="w2_raw")
        gate_sb = [keep.tile([P, T], F32, name="gate%d" % r) for r in range(2)]
        y = keep.tile([P, S], F32, name="y")
        warm = keep.tile([P, 8], F32, name="warm")
        warm_out = keep.tile([P, 8], F32, name="warm_out")

        nc.vector.memset(xs[:].bitcast(I32), 0)
        nc.gpsimd.memset(warm[:], 0.0)
        nc.scalar.activation(warm_out[:], warm[:], SILU)

        def placed(offset, shape, dtype, name):
            return arena.tile(shape, dtype, name=name, offset=offset, align_bytes=64)

        def slot_at(s, g=0):
            return s * SLOT_BYTES + g * PASS_BYTES

        def stage_at(s, g):
            return (E + 1) * SLOT_BYTES + ((s * PASSES + g) % STAGES) * STAGE_BYTES

        used = {}
        w2_at = {}

        def after(where, shape, dtype, size, name):
            if where is None:
                return keep.tile(shape, dtype, name=name, align_bytes=64)
            if where[0] == "w":
                return placed(w2_at[where[1]], shape, dtype, name)
            at = used.get(where, 0)
            if name.startswith("w2_bf"):
                w2_at[int(name[-1])] = slot_at(where[0], where[1]) + at
            used[where] = at + shape[1] * size
            assert used[where] <= PASS_BYTES
            return placed(slot_at(where[0], where[1]) + at, shape, dtype, name)

        w1_raw = {}

        def load_w1_pass(s, g):
            raw = placed(slot_at(s, g), [P, PACK, H], F32, "w1_raw_%d_%d" % (s, g))
            rows = w1[ORDER[s], g * K_PASS:(g + 1) * K_PASS, :]
            nc.sync.dma_start(out=raw[:], in_=rows.rearrange("(p j) c -> p j c", j=PACK))
            w1_raw[(s, g)] = raw[:]

        def load_w1(s):
            raw = placed(slot_at(s), [P, PASSES, PACK, H], F32, "w1_raw_%d" % s)
            nc.sync.dma_start(out=raw[:], in_=w1[ORDER[s]].rearrange("(g p j) c -> p g j c", g=PASSES, j=PACK))
            for g in range(PASSES):
                w1_raw[(s, g)] = raw[:, g]

        def load_w2(e0, e1):
            nc.sync.dma_start(out=w2_raw[:, e0:e1], in_=w2[e0:e1].rearrange("e (p j) n -> p e j n", j=PACK))

        def load_gate(r):
            nc.sync.dma_start(out=gate_sb[r][:], in_=gate[r])

        def load_x(g):
            nc.sync.dma_start(out=xw[g][:], in_=x_words[g].rearrange("p t r -> p (t r)").bitcast(I32))

        def load_scales():
            for q in range(4):
                nc.sync.dma_start(out=xs[32 * q:32 * q + 4 * PASSES, :].bitcast(I32), in_=x_scales[:, 4 * q:4 * q + 4, :].bitcast(I32))

        def load_pos():
            nc.sync.dma_start(pos_sb[0][:], pos1)
            nc.sync.dma_start(pos_sb[1][:], pos2)

        for name in LOADS:
            if name == "o":
                nc.sync.dma_start(offs_sb[:], offs)
            elif name == "s":
                load_scales()
            elif name == "p":
                load_pos()
            elif name[0] == "x":
                load_x(int(name[1]))
            elif name[0] == "g":
                half = {"": slice(0, T), "a": slice(0, T // 2), "b": slice(T // 2, T)}[name[2:]]
                nc.sync.dma_start(out=gate_sb[int(name[1])][:, half], in_=gate[int(name[1])][:, half])
            elif name[0] == "v":
                load_w2(int(name[1]), int(name[2]))
            elif int(name[1]) in WHOLE:
                if name[2] == "1":
                    load_w1(int(name[1]))
            else:
                load_w1_pass(int(name[1]), int(name[2]))

        slots = {}
        w1_q = {}
        w1_bf = {}
        w2_bf = {}
        w2_q = {}
        h_bf = {}
        h_q = {}

        def gather_tokens(e):
            lst = offs_sb[:, e * C // LIST_ROWS:(e + 1) * C // LIST_ROWS]
            gw = [after(GATHER_AFTER[e], [P, C], U32, 4, "gw%d_%d" % (g, e)) for g in range(PASSES)]
            gs = after(GATHER_AFTER[e], [P, C], U8, 1, "gs_%d" % e)
            for g in range(PASSES):
                nc.vector.tensor_copy(gw[g][:], xw[g][:].bitcast(U32).indirect(lst))
            nc.vector.tensor_copy(gs[:], xs[:].indirect(lst))
            slots[e] = (gw, gs)

        def round_w1(e, g):
            rounded = placed(stage_at(e, g), [P, H * PACK], BF16, "w1_bf_%d_%d" % (e, g))
            dst = rounded[:].rearrange("p (t m a b) -> p m a t b", t=PACK, a=2, b=2)
            src = w1_raw[(e, g)].rearrange("p (a b) (m t) -> p m a t b", t=PACK, b=2)
            ms = SCALAR_M[e][g]
            if ms > 0:
                nc.scalar.copy(dst[:, :ms], src[:, :ms])
            if ms < P:
                nc.vector.tensor_copy(dst[:, ms:], src[:, ms:])
            w1_bf[(e, g)] = rounded

        def quantise_w1(e, g):
            if g == 0:
                w1_q[e] = (ring.tile([P, PASSES, H], U32, name="w1_codes", align_bytes=64, bufs=2),
                           ring.tile([P, PASSES, H], U8, name="w1_scales", align_bytes=64, bufs=2))
            codes, scales = w1_q[e]
            nc.vector.quantize_mx(out=codes[:, g, :].bitcast(FP8X4), scales=scales[:, g, :], in_=w1_bf[(e, g)][:])

        def round_w2(e):
            rounded = after(W2_AFTER[e], [P, N * PACK], BF16, 2, "w2_bf_%d" % e)
            dst = rounded[:].rearrange("p (c i a b) -> p c a i b", i=4, a=2, b=2)
            src = w2_raw[:, e].rearrange("p (a b) (c i) -> p c a i b", i=4, b=2)
            (nc.scalar.copy if W2_SCALAR[e] else nc.vector.tensor_copy)(dst, src)
            w2_bf[e] = rounded

        def quantise_w2(e):
            codes = keep.tile([P, N], U32, name="w2_codes_%d" % e, align_bytes=64)
            scales = keep.tile([P, N], U8, name="w2_scales_%d" % e, align_bytes=64)
            nc.vector.quantize_mx(out=codes[:].bitcast(FP8X4), scales=scales[:], in_=w2_bf[e][:])
            w2_q[e] = (codes, scales)

        def first_layer(e, words, planes, c0, h):
            w_codes, w_scales = w1_q[e]
            for u in range(C // GROUP):
                cols = slice(c0 + u * GROUP, c0 + (u + 1) * GROUP)
                acc = ps1.tile([P, PACK, GROUP], F32, name="acc1")
                if e in ONE:
                    order = [(g, t, g == 0 and t == 0, g == PASSES - 1 and t == PACK - 1) for g in range(PASSES) for t in range(PACK)]
                else:
                    order = [(g, t, g == 0, g == PASSES - 1) for t in range(PACK) for g in range(PASSES)]
                for g, t, first, last in order:
                    ch = slice(t * P, (t + 1) * P)
                    nc.tensor.matmul_mx(
                        out=acc[:, t, :],
                        lhsT=w_codes[:, g, ch].bitcast(FP8X4), lhsT_scale=w_scales[:, g, ch],
                        rhs=words[g][:, cols].bitcast(FP8X4), rhs_scale=planes[4 * g:, cols],
                        start=first, stop=last,
                    )
                nc.scalar.activation(
                    h[:, u * GROUP * PACK:(u + 1) * GROUP * PACK].rearrange("p (n t) -> p n t", t=PACK),
                    acc[:].rearrange("p t n -> p n t"), SILU)

        def quantise_h(h, where, name):
            codes = after(where, [P, C], U32, 4, "h_codes_" + name)
            scales = after(where, [P, C], U8, 1, "h_scales_" + name)
            nc.vector.quantize_mx(out=codes[:].bitcast(FP8X4), scales=scales[:], in_=h[:])
            return codes, scales

        def second_layer(e, h_codes, h_scales):
            w_codes, w_scales = w2_q[e]
            acc = ps2.tile([P, C], F32, name="acc2")
            nc.tensor.matmul_mx(out=acc[:], lhsT=w_codes[:].bitcast(FP8X4), lhsT_scale=w_scales[:],
                                rhs=h_codes[:].bitcast(FP8X4), rhs_scale=h_scales[:], start=True, stop=True)
            return acc

        sh = ORDER.index(E)
        units = [(ORDER.index(e), e, 0) for e in range(E)] + [(sh, E, c) for c in range(T // C)]
        todo = []
        for u, (s, e, c) in enumerate(units):
            todo.append(("first", u))
            todo.append(("hq", u))
            if e < E:
                todo.append(("second", u))
        todo = sorted(todo, key=lambda x: (units[x[1]][0], x[1]))
        w2_todo = list(range(E + 1))
        g_todo = list(range(E))

        def emit(now):
            rounded = []
            again = True
            while again:
                again = False
                for item in list(todo):
                    kind, u = item
                    s, e, c = units[u]
                    if kind == "first":
                        w = H_AFTER[u]
                        if (s, 1) <= now and (w is None or (w[1] in w2_q if w[0] == "w" else w <= now)) and (e == E or e in slots):
                            if w is None:
                                h = ring.tile([P, C * PACK], BF16, name="h_bf", align_bytes=64)
                            else:
                                h = after(w, [P, C * PACK], BF16, 2, "h_bf_%d" % u)
                            if e < E:
                                first_layer(s, slots[e][0], slots[e][1], 0, h)
                            else:
                                first_layer(s, xw, xs, c * C, h)
                            h_bf[u] = h
                            todo.remove(item)
                            again = True
                    elif kind == "hq":
                        w = Q_AFTER[u]
                        if u in h_bf and w <= now:
                            h_q[u] = quantise_h(h_bf[u], w, "%d" % u)
                            todo.remove(item)
                            again = True
                    elif u in h_q and e in w2_q:
                        acc = second_layer(e, h_q[u][0], h_q[u][1])
                        nc.scalar.copy(y[:, e * C:(e + 1) * C], acc[:])
                        todo.remove(item)
                        again = True
                for e in list(w2_todo):
                    if W2_AFTER[e] <= now:
                        round_w2(e)
                        rounded.append(e)
                        w2_todo.remove(e)
                for e in list(g_todo):
                    if GATHER_AFTER[e] is None or GATHER_AFTER[e] <= now:
                        gather_tokens(e)
                        g_todo.remove(e)
                        again = True
                for e in rounded:
                    quantise_w2(e)
                    again = True
                rounded = []

        emit((-1, 0))
        for s in range(E + 1):
            round_w1(s, 0)
            round_w1(s, 1)
            quantise_w1(s, 0)
            emit((s, 0))
            quantise_w1(s, 1)
            emit((s, 1))
        assert not todo and not w2_todo and not g_todo

        picked = [placed(slot_at(5, r), [P, T], F32, "picked%d" % r) for r in range(2)]
        partial = placed(slot_at(5, 0) + 4096, [P, T], F32, "partial")
        result = placed(slot_at(5, 1) + 4096, [P, T], F32, "result")

        def pick(r, c0, c1):
            cols = slice(c0, c1)
            nc.vector.tensor_tensor(picked[r][:, cols], y[:].indirect(pos_sb[r][:, c0 // LIST_ROWS:c1 // LIST_ROWS]), gate_sb[r][:, cols], MULT)

        for c in range(T // C):
            cols = slice(c * C, (c + 1) * C)
            if c % PICK0 == 0:
                wide = slice(c * C, (c + PICK0) * C)
                pick(0, wide.start, wide.stop)
                pick(1, wide.start, wide.stop)
                nc.vector.tensor_tensor(partial[:, wide], picked[0][:, wide], picked[1][:, wide], ADD)
            acc = second_layer(E, h_q[E + c][0], h_q[E + c][1])
            nc.vector.tensor_tensor(result[:, cols], acc[:], partial[:, cols], ADD)
            if c in LAST:
                first = (max([x for x in LAST if x < c] + [-1]) + 1) * C
                nc.sync.dma_start(out=out[:, first:cols.stop], in_=result[:, first:cols.stop])
